import numpy as np
import ml_dtypes


def mxq(x, axis, fmt="e4m3"):
    dtype, down = {"e4m3": (ml_dtypes.float8_e4m3fn, 7), "e5m2": (ml_dtypes.float8_e5m2, 14)}[fmt]
    v = np.moveaxis(np.asarray(x, np.float32).astype(ml_dtypes.bfloat16).astype(np.float64), axis, -1)
    blocks = v.reshape(v.shape[:-1] + (-1, 32))
    amax = np.abs(blocks).max(-1, keepdims=True)
    byte = np.maximum(np.where(amax > 0, np.frexp(amax)[1] - 1 + 127, 0) - down, 1)
    scale = np.exp2(byte - 127.0)
    codes = (blocks / scale).astype(np.float32).astype(dtype).astype(np.float64)
    return np.moveaxis((codes * scale).reshape(v.shape), -1, axis)


WIDE = False


def mx_kscale(k):
    if not WIDE:
        return np.ones(k)
    levels = np.array([10, -10, 5, -5, 0])
    if k % 512:
        return np.exp2(np.random.permutation(np.resize(levels, k // 32))).repeat(32)
    a = np.empty((k // 512, 16))
    for p in range(k // 512):
        a[p, :8] = np.random.permutation(np.resize(levels, 8))
        for g in range(8):
            far = levels[np.abs(levels - a[p, g]) >= 10]
            a[p, g + 8] = far[np.random.randint(len(far))]
    return np.exp2(a.ravel()).repeat(32)


def f64(x):
    return np.asarray(x).astype(np.float64)


def striped8(idx):
    return np.asarray(idx).reshape(8, -1, 16).transpose(0, 2, 1).reshape(128, -1).astype(np.uint16)


def unstriped8(offs):
    return offs.reshape(8, 16, -1).transpose(0, 2, 1).reshape(8, -1).astype(np.int64)


def pick8(x, idx, run):
    r = np.arange(len(x))
    return x[r[:, None], idx[r % (8 * run) // run]]


E2M1 = np.array([0.0, 0.5, 1.0, 1.5, 2.0, 3.0, 4.0, 6.0, -0.0, -0.5, -1.0, -1.5, -2.0, -3.0, -4.0, -6.0])


def pack_weight(w, fmt):
    k, n = w.shape
    w = f64(np.asarray(w, np.float32).astype(ml_dtypes.bfloat16)).reshape(k // 32, 32, n)
    amax = np.abs(w).max(1)
    if fmt == "e4m3":
        byte = np.frexp(amax)[1] - 1 + 127 - 7
    else:
        mant, ex = np.frexp(amax / 6.0)
        byte = np.where(mant > 0.5, ex, ex - 1) + 127
    byte = np.clip(np.where(amax > 0, byte, 1), 1, 254)
    scaled = (w * np.exp2(127.0 - byte)[:, None, :]).reshape(k, n).astype(np.float32)
    by_word = np.ascontiguousarray(scaled.reshape(k // 512, 128, 4, n).transpose(0, 1, 3, 2))
    if fmt == "e4m3":
        words = by_word.astype(ml_dtypes.float8_e4m3fn).view(np.uint8)
    else:
        c = by_word.astype(ml_dtypes.float4_e2m1fn).view(np.uint8) & 0xF
        words = (c[..., 0::2] | (c[..., 1::2] << 4)).reshape(k // 512, 128, 2 * n)
    return np.ascontiguousarray(words), np.ascontiguousarray(byte.astype(np.uint8).reshape(k // 512, 16, n))


def unpack_weight(words, scales, fmt):
    g, _, n = scales.shape
    words = np.ascontiguousarray(words).reshape(g, 128, n, -1)
    if fmt == "e4m3":
        vals = words.view(ml_dtypes.float8_e4m3fn).astype(np.float64)
    else:
        nib = np.empty((g, 128, n, 4), np.uint8)
        nib[..., 0::2] = words & 0xF
        nib[..., 1::2] = words >> 4
        vals = E2M1[nib]
    vals = vals * np.repeat(np.exp2(scales.astype(np.float64) - 127.0), 8, axis=1)[..., None]
    return vals.transpose(0, 1, 3, 2).reshape(g * 512, n)


D, T, Q, I, E = 512, 1024, 128, 512, 512


def setup_inputs():
    n = np.random.standard_normal
    idx = np.stack([np.random.permutation(T)[:I] for _ in range(8)])
    idx2 = np.stack([np.random.permutation(T)[:I] for _ in range(8)])
    fd = mx_kscale(D)
    ft = mx_kscale(T)
    keysp = pack_weight(n((D, T)) / fd[:, None], "e4m3")
    return {
        "query": (n((D, Q)) * 0.3 / np.sqrt(D) * fd[:, None]).astype(np.float32),
        "keys_words": keysp[0],
        "keys_scales": keysp[1],
        "lam": (np.random.uniform(0.3, 1.2, (Q, 1))).astype(np.float32),
        "share": (np.random.uniform(0.3, 1.0, (Q, 1))).astype(np.float32),
        "fac": (np.random.uniform(4.0, 16.0, (1, T)) * ft).astype(np.float32),
        "vals": (n((T, E)) / ft[:, None]).astype(np.float32),
        "offs": striped8(idx),
        "offs2": striped8(idx2),
    }


def reference(query, keys_words, keys_scales, lam, share, fac, vals, offs, offs2):
    idx = unstriped8(offs)
    idx2 = unstriped8(offs2)
    keysu = unpack_weight(keys_words, keys_scales, "e4m3")
    queryq = mxq(f64(query), 0, "e4m3")
    a = queryq.T @ keysu
    s = pick8(a, idx, 16) + pick8(a, idx2, 16) * f64(lam)
    p = np.exp(s - np.max(s, axis=1, keepdims=True))
    w = p / np.sum(p, axis=1, keepdims=True)
    wa = np.zeros((Q, T))
    wa[np.arange(Q)[:, None], idx[np.arange(Q) % 128 // 16]] = w
    wb = np.zeros((Q, T))
    wb[np.arange(Q)[:, None], idx2[np.arange(Q) % 128 // 16]] = w
    wg = (wa + wb * f64(share)) * f64(fac)
    wt = wg.T
    wtq = mxq(wt, 0, "e4m3")
    valsq = mxq(f64(vals), 0, "e4m3")
    o = wtq.T @ valsq
    return o

@@ -1,0 +1,207 @@
+from contextlib import ExitStack
+
+import concourse.mybir as mybir
+from concourse.masks import make_identity
+
+F32 = mybir.dt.float32
+BF16 = mybir.dt.bfloat16
+I32 = mybir.dt.int32
+U32 = mybir.dt.uint32
+U16 = mybir.dt.uint16
+U8 = mybir.dt.uint8
+FP8X4 = mybir.dt.float8_e4m3fn_x4
+ALU = mybir.AluOpType
+ACT = mybir.ActivationFunctionType
+AX = mybir.AxisListType
+
+D, T, Q, SLOTS, E = 512, 1024, 128, 512, 512
+P = 128
+PACK = 4
+K_PASS = P * PACK
+PASSES = T // K_PASS
+CHUNK = 256
+HEAD = 128
+FLOPS = 2 * D * Q * T + 2 * T * Q * E
+
+
+def tile_attend_pairreads_heads_kernel(tc, query, keys_words, keys_scales, lam, share, fac, vals, offs, offs2, out):
+    nc = tc.nc
+    with ExitStack() as ctx:
+        lists = ctx.enter_context(tc.tile_pool(name="lists", bufs=1))
+        sb = ctx.enter_context(tc.tile_pool(name="sb", bufs=1))
+        psum = ctx.enter_context(tc.psum_pool(name="psum", bufs=1))
+
+        def tile(name, shape, dtype, tag=None):
+            return sb.tile(shape, dtype, name=name, tag=tag or name, align_bytes=64)
+
+        k_scales = tile("k_scales", [P, CHUNK], U8)
+        nc.vector.memset(k_scales[:].bitcast(I32), 0)
+        q_raw = tile("q_raw", [P, PACK, Q], F32)
+        nc.sync.dma_start(q_raw[:], query.rearrange("(p j) q -> p j q", j=PACK))
+        for quad in range(4):
+            rows = keys_scales[0, 4 * quad : 4 * quad + 4, :].bitcast(I32)
+            nc.scalar.dma_start(
+                k_scales[32 * quad : 32 * quad + 16, :].bitcast(I32),
+                rows.rearrange("r (c n) -> c r n", c=T // CHUNK),
+            )
+        words = keys_words[0].rearrange("p n t -> p (n t)").bitcast(I32)
+        k_words = []
+        for h in range(2):
+            kw = tile("k_words%d" % h, [P, T // 2], U32)
+            nc.sync.dma_start(kw[:].bitcast(I32), words[:, h * (T // 2) : (h + 1) * (T // 2)])
+            k_words.append(kw)
+        lam_col = tile("lam_col", [P, 1], F32)
+        nc.sync.dma_start(lam_col[:], lam)
+        list2 = lists.tile([P, SLOTS // 16], U16, name="list2")
+        nc.sync.dma_start(list2[:], offs2)
+        v_raw = {}
+
+        def load_vals(g, h):
+            v_raw[g, h] = tile("v_raw%d%d" % (g, h), [P, PACK, CHUNK], F32)
+            part = vals[g * K_PASS : (g + 1) * K_PASS, h * CHUNK : (h + 1) * CHUNK]
+            nc.sync.dma_start(v_raw[g, h][:], part.rearrange("(p j) e -> p j e", j=PACK))
+
+        list1 = lists.tile([P, SLOTS // 16], U16, name="list1")
+        nc.sync.dma_start(list1[:], offs)
+        load_vals(0, 0)
+        load_vals(0, 1)
+        load_vals(1, 0)
+        load_vals(1, 1)
+        share_col = tile("share_col", [P, 1], F32)
+        nc.sync.dma_start(share_col[:], share)
+        fac_t = tile("fac_t", [P, PASSES, PACK], F32)
+        nc.sync.dma_start(fac_t[:], fac[0].rearrange("(g p j) -> p g j", g=PASSES, j=PACK))
+
+        warm = tile("warm", [P, 2], F32)
+        nc.vector.memset(warm[:, 0:1], 0.0)
+        nc.scalar.activation(warm[:, 1:2], warm[:, 0:1], ACT.Exp)
+        wa = tile("wa", [P, T], F32)
+        wb = tile("wb", [P, T], F32)
+        nc.vector.memset(wa[:], 0.0)
+        nc.vector.memset(wb[:], 0.0)
+        ident = tile("ident", [P, P], F32)
+        make_identity(nc, ident[:])
+
+        q_bf = tile("q_bf", [P, Q, PACK], BF16)
+        nc.vector.tensor_copy(q_bf[:], q_raw[:].rearrange("p j q -> p q j"))
+        q_codes = tile("q_codes", [P, Q], U32)
+        q_scales = tile("q_scales", [P, Q], U8)
+        nc.vector.quantize_mx(q_codes[:].bitcast(FP8X4), q_scales[:], q_bf[:].rearrange("p q j -> p (q j)"))
+        lam_wide = tile("lam_wide", [P, SLOTS], F32)
+        nc.scalar.copy(lam_wide[:], lam_col[:].to_broadcast([P, SLOTS]))
+
+        a = tile("a", [P, T], F32)
+        for c in range(T // CHUNK):
+            bank = psum.tile([P, CHUNK], F32, name="a_bank%d" % c)
+            cols = slice((c % 2) * CHUNK, (c % 2 + 1) * CHUNK)
+            nc.tensor.matmul_mx(
+                bank[:],
+                lhsT=q_codes[:].bitcast(FP8X4),
+                lhsT_scale=q_scales[:],
+                rhs=k_words[c // 2][:, cols].bitcast(FP8X4),
+                rhs_scale=k_scales[4 * c : P, :],
+                start=True,
+                stop=True,
+            )
+            if c % 2 == 0:
+                nc.vector.tensor_copy(a[:, c * CHUNK : (c + 1) * CHUNK], bank[:])
+            else:
+                nc.scalar.copy(a[:, c * CHUNK : (c + 1) * CHUNK], bank[:])
+
+        def interleave_vals(dst, g, h):
+            nc.scalar.copy(
+                dst.rearrange("p (c i) j -> p c j i", i=4),
+                v_raw[g, h][:].rearrange("p j (c i) -> p c j i", i=4),
+            )
+
+        v_first = tile("v_first", [P, CHUNK, PACK], BF16, "k_words1")
+        interleave_vals(v_first[:], 0, 0)
+
+        half = SLOTS // 2
+        halves = [(slice(u * half, (u + 1) * half), slice(u * half // 16, (u + 1) * half // 16)) for u in range(2)]
+        second = tile("second", [P, SLOTS], F32)
+        s = tile("s", [P, SLOTS], F32)
+        for cols, entries in halves:
+            nc.vector.tensor_tensor(second[:, cols], a[:].indirect(list2[:, entries]), lam_wide[:, cols], ALU.mult)
+        for cols, entries in halves:
+            nc.vector.tensor_tensor(s[:, cols], a[:].indirect(list1[:, entries]), second[:, cols], ALU.add)
+        neg_max = tile("neg_max", [P, 1], F32)
+        nc.vector.tensor_reduce(neg_max[:], s[:], AX.X, ALU.max, negate=True)
+        v_codes0 = tile("v_codes0", [P, CHUNK], U32, "second")
+        v_scales0 = tile("v_scales0", [P, CHUNK], U8)
+        nc.vector.quantize_mx(v_codes0[:].bitcast(FP8X4), v_scales0[:], v_first[:].rearrange("p e j -> p (e j)"))
+
+        p_head = tile("p_head", [P, HEAD], F32, "v_raw00")
+        nc.scalar.activation(p_head[:], s[:, 0:HEAD], ACT.Exp, bias=neg_max[:])
+        p = tile("p", [P, SLOTS], F32)
+        total = tile("total", [P, 1], F32)
+        nc.scalar.activation(p[:], s[:], ACT.Exp, bias=neg_max[:], accum_out=total[:])
+        v_rest = tile("v_rest", [P, 3 * CHUNK, PACK], BF16, "s")
+        interleave_vals(v_rest[:, 0:CHUNK], 0, 1)
+        interleave_vals(v_rest[:, CHUNK : 2 * CHUNK], 1, 0)
+
+        rinv = tile("rinv", [P, 1], F32)
+        nc.vector.tensor_copy(wa[:].indirect(list1[:, 0 : HEAD // 16]), p_head[:])
+        nc.vector.tensor_copy(wb[:].indirect(list2[:, 0 : HEAD // 16]), p_head[:])
+        nc.vector.reciprocal(rinv[:], total[:])
+        nc.vector.tensor_copy(wa[:].indirect(list1[:, HEAD // 16 : SLOTS // 16]), p[:, HEAD:SLOTS])
+        nc.vector.tensor_copy(wb[:].indirect(list2[:, HEAD // 16 : SLOTS // 16]), p[:, HEAD:SLOTS])
+        rshare = tile("rshare", [P, 1], F32)
+        nc.scalar.activation(rshare[:], rinv[:], ACT.Copy, scale=share_col[:])
+
+        def by_place(window, g):
+            return window[:, g * K_PASS : (g + 1) * K_PASS].rearrange("q (p j) -> q j p", j=PACK)
+
+        wa_dealt = tile("wa_dealt", [P, PASSES, PACK, P], F32, "v_raw10")
+        wt_banks = [psum.tile([P, PACK, Q], F32, name="wt_bank%d" % g) for g in range(PASSES)]
+        for g in range(PASSES):
+            nc.scalar.activation(wa_dealt[:, g], by_place(wa, g), ACT.Copy, scale=rinv[:])
+            for j in range(PACK):
+                nc.tensor.matmul(wt_banks[g][:, j, :], wa_dealt[:, g, j, :], ident[:], is_transpose=True, start=(j == 0), stop=False)
+        interleave_vals(v_rest[:, 2 * CHUNK : 3 * CHUNK], 1, 1)
+
+        wb_dealt = [tile("wb_dealt0", [P, PACK, P], F32), tile("wb_dealt1", [P, PACK, P], F32, "v_raw11")]
+        nc.vector.tensor_scalar(wb_dealt[0][:], by_place(wb, 0), rshare[:], None, ALU.mult)
+        nc.scalar.activation(wb_dealt[1][:], by_place(wb, 1), ACT.Copy, scale=rshare[:])
+        for g in range(PASSES):
+            for j in range(PACK):
+                nc.tensor.matmul(wt_banks[g][:, j, :], wb_dealt[g][:, j, :], ident[:], is_transpose=True, start=False, stop=(j == PACK - 1))
+
+        v_codes1 = tile("v_codes1", [P, 3 * CHUNK], U32, "p")
+        v_scales1 = tile("v_scales1", [P, 3 * CHUNK], U8)
+        for lo, hi in ((0, CHUNK), (CHUNK, 3 * CHUNK)):
+            nc.vector.quantize_mx(v_codes1[:, lo:hi].bitcast(FP8X4), v_scales1[:, lo:hi], v_rest[:, lo:hi].rearrange("p e j -> p (e j)"))
+        v_parts = [(v_codes0[:], v_scales0[:])] + [
+            (v_codes1[:, n * CHUNK : (n + 1) * CHUNK], v_scales1[:, n * CHUNK : (n + 1) * CHUNK]) for n in range(3)
+        ]
+
+        wt_bf = [tile("wt_bf%d" % g, [P, Q, PACK], BF16) for g in range(PASSES)]
+        for g in range(PASSES):
+            nc.vector.tensor_tensor(
+                wt_bf[g][:],
+                wt_banks[g][:].rearrange("p j q -> p q j"),
+                fac_t[:, g, :].unsqueeze(1).to_broadcast([P, Q, PACK]),
+                ALU.mult,
+            )
+        w_codes = [tile("w_codes%d" % g, [P, Q], U32) for g in range(PASSES)]
+        w_scales = [tile("w_scales%d" % g, [P, Q], U8) for g in range(PASSES)]
+        out_banks = [psum.tile([P, CHUNK], F32, name="out_bank%d" % h) for h in range(2)]
+        for g in range(PASSES):
+            nc.vector.quantize_mx(w_codes[g][:].bitcast(FP8X4), w_scales[g][:], wt_bf[g][:].rearrange("p q j -> p (q j)"))
+            for h in range(2):
+                codes, scales = v_parts[2 * g + h]
+                nc.tensor.matmul_mx(
+                    out_banks[h][:],
+                    lhsT=w_codes[g][:].bitcast(FP8X4),
+                    lhsT_scale=w_scales[g][:],
+                    rhs=codes.bitcast(FP8X4),
+                    rhs_scale=scales,
+                    start=(g == 0),
+                    stop=(g == PASSES - 1),
+                )
+        res0 = tile("res0", [P, CHUNK], F32)
+        nc.scalar.copy(res0[:], out_banks[0][:])
+        nc.scalar.dma_start(out[:, 0:CHUNK], res0[:])
+        res1 = tile("res1", [P, CHUNK], F32)
+        nc.vector.tensor_copy(res1[:], out_banks[1][:])
+        nc.sync.dma_start(out[:, CHUNK:E], res1[:])

@@ -83,7 +83,10 @@ def tile_attend_pairreads_heads_kernel(tc, query, keys_words, keys_scales, lam, 
         make_identity(nc, ident[:])
 
         q_bf = tile("q_bf", [P, Q, PACK], BF16)
-        nc.vector.tensor_copy(q_bf[:], q_raw[:].rearrange("p j q -> p q j"))
+        nc.vector.tensor_copy(
+            q_bf[:].rearrange("p (c i) j -> p c j i", i=4),
+            q_raw[:].rearrange("p j (c i) -> p c j i", i=4),
+        )
         q_codes = tile("q_codes", [P, Q], U32)
         q_scales = tile("q_scales", [P, Q], U8)
         nc.vector.quantize_mx(q_codes[:].bitcast(FP8X4), q_scales[:], q_bf[:].rearrange("p q j -> p (q j)"))
@@ -131,18 +134,18 @@ def tile_attend_pairreads_heads_kernel(tc, query, keys_words, keys_scales, lam, 
         v_scales0 = tile("v_scales0", [P, CHUNK], U8)
         nc.vector.quantize_mx(v_codes0[:].bitcast(FP8X4), v_scales0[:], v_first[:].rearrange("p e j -> p (e j)"))
 
-        p_head = tile("p_head", [P, HEAD], F32, "v_raw00")
-        nc.scalar.activation(p_head[:], s[:, 0:HEAD], ACT.Exp, bias=neg_max[:])
-        p = tile("p", [P, SLOTS], F32)
+        p_both = tile("p_both", [P, HEAD + SLOTS], F32, "v_raw00")
+        p_head, p = p_both[:, 0:HEAD], p_both[:, HEAD : HEAD + SLOTS]
+        nc.scalar.activation(p_head, s[:, 0:HEAD], ACT.Exp, bias=neg_max[:])
         total = tile("total", [P, 1], F32)
-        nc.scalar.activation(p[:], s[:], ACT.Exp, bias=neg_max[:], accum_out=total[:])
+        nc.scalar.activation(p, s[:], ACT.Exp, bias=neg_max[:], accum_out=total[:])
         v_rest = tile("v_rest", [P, 3 * CHUNK, PACK], BF16, "s")
         interleave_vals(v_rest[:, 0:CHUNK], 0, 1)
         interleave_vals(v_rest[:, CHUNK : 2 * CHUNK], 1, 0)
 
         rinv = tile("rinv", [P, 1], F32)
-        nc.vector.tensor_copy(wa[:].indirect(list1[:, 0 : HEAD // 16]), p_head[:])
-        nc.vector.tensor_copy(wb[:].indirect(list2[:, 0 : HEAD // 16]), p_head[:])
+        nc.vector.tensor_copy(wa[:].indirect(list1[:, 0 : HEAD // 16]), p_head)
+        nc.vector.tensor_copy(wb[:].indirect(list2[:, 0 : HEAD // 16]), p_head)
         nc.vector.reciprocal(rinv[:], total[:])
         nc.vector.tensor_copy(wa[:].indirect(list1[:, HEAD // 16 : SLOTS // 16]), p[:, HEAD:SLOTS])
         nc.vector.tensor_copy(wb[:].indirect(list2[:, HEAD // 16 : SLOTS // 16]), p[:, HEAD:SLOTS])
@@ -150,24 +153,27 @@ def tile_attend_pairreads_heads_kernel(tc, query, keys_words, keys_scales, lam, 
         nc.scalar.activation(rshare[:], rinv[:], ACT.Copy, scale=share_col[:])
 
         def by_place(window, g):
-            return window[:, g * K_PASS : (g + 1) * K_PASS].rearrange("q (p j) -> q j p", j=PACK)
+            return window[:, g * K_PASS : (g + 1) * K_PASS].rearrange("q (c i j) -> q c j i", i=4, j=PACK)
+
+        def by_line(dealt):
+            return dealt.rearrange("q j (c i) -> q c j i", i=4)
 
         wa_dealt = tile("wa_dealt", [P, PASSES, PACK, P], F32, "v_raw10")
         wt_banks = [psum.tile([P, PACK, Q], F32, name="wt_bank%d" % g) for g in range(PASSES)]
         for g in range(PASSES):
-            nc.scalar.activation(wa_dealt[:, g], by_place(wa, g), ACT.Copy, scale=rinv[:])
+            nc.scalar.activation(by_line(wa_dealt[:, g]), by_place(wa, g), ACT.Copy, scale=rinv[:])
             for j in range(PACK):
                 nc.tensor.matmul(wt_banks[g][:, j, :], wa_dealt[:, g, j, :], ident[:], is_transpose=True, start=(j == 0), stop=False)
         interleave_vals(v_rest[:, 2 * CHUNK : 3 * CHUNK], 1, 1)
 
         wb_dealt = [tile("wb_dealt0", [P, PACK, P], F32), tile("wb_dealt1", [P, PACK, P], F32, "v_raw11")]
-        nc.vector.tensor_scalar(wb_dealt[0][:], by_place(wb, 0), rshare[:], None, ALU.mult)
-        nc.scalar.activation(wb_dealt[1][:], by_place(wb, 1), ACT.Copy, scale=rshare[:])
+        nc.vector.tensor_scalar(by_line(wb_dealt[0][:]), by_place(wb, 0), rshare[:], None, ALU.mult)
+        nc.scalar.activation(by_line(wb_dealt[1][:]), by_place(wb, 1), ACT.Copy, scale=rshare[:])
         for g in range(PASSES):
             for j in range(PACK):
                 nc.tensor.matmul(wt_banks[g][:, j, :], wb_dealt[g][:, j, :], ident[:], is_transpose=True, start=False, stop=(j == PACK - 1))
 
-        v_codes1 = tile("v_codes1", [P, 3 * CHUNK], U32, "p")
+        v_codes1 = tile("v_codes1", [P, 3 * CHUNK], U32, "v_raw00")
         v_scales1 = tile("v_scales1", [P, 3 * CHUNK], U8)
         for lo, hi in ((0, CHUNK), (CHUNK, 3 * CHUNK)):
             nc.vector.quantize_mx(v_codes1[:, lo:hi].bitcast(FP8X4), v_scales1[:, lo:hi], v_rest[:, lo:hi].rearrange("p e j -> p (e j)"))

@@ -21,6 +21,7 @@ K_PASS = P * PACK
 PASSES = T // K_PASS
 CHUNK = 256
 HEAD = 128
+V_CUTS = ((0, CHUNK, E), (0, 352, E))
 FLOPS = 2 * D * Q * T + 2 * T * Q * E
 
 
@@ -38,6 +39,8 @@ def tile_attend_pairreads_heads_kernel(tc, query, keys_words, keys_scales, lam, 
         nc.vector.memset(k_scales[:].bitcast(I32), 0)
         q_raw = tile("q_raw", [P, PACK, Q], F32)
         nc.sync.dma_start(q_raw[:], query.rearrange("(p j) q -> p j q", j=PACK))
+        lam_col = tile("lam_col", [P, 1], F32)
+        nc.sync.dma_start(lam_col[:], lam)
         for quad in range(4):
             rows = keys_scales[0, 4 * quad : 4 * quad + 4, :].bitcast(I32)
             nc.scalar.dma_start(
@@ -50,15 +53,14 @@ def tile_attend_pairreads_heads_kernel(tc, query, keys_words, keys_scales, lam, 
             kw = tile("k_words%d" % h, [P, T // 2], U32)
             nc.sync.dma_start(kw[:].bitcast(I32), words[:, h * (T // 2) : (h + 1) * (T // 2)])
             k_words.append(kw)
-        lam_col = tile("lam_col", [P, 1], F32)
-        nc.sync.dma_start(lam_col[:], lam)
         list2 = lists.tile([P, SLOTS // 16], U16, name="list2")
         nc.sync.dma_start(list2[:], offs2)
         v_raw = {}
 
         def load_vals(g, h):
-            v_raw[g, h] = tile("v_raw%d%d" % (g, h), [P, PACK, CHUNK], F32)
-            part = vals[g * K_PASS : (g + 1) * K_PASS, h * CHUNK : (h + 1) * CHUNK]
+            lo, hi = V_CUTS[g][h], V_CUTS[g][h + 1]
+            v_raw[g, h] = tile("v_raw%d%d" % (g, h), [P, PACK, hi - lo], F32)
+            part = vals[g * K_PASS : (g + 1) * K_PASS, lo:hi]
             nc.sync.dma_start(v_raw[g, h][:], part.rearrange("(p j) e -> p j e", j=PACK))
 
         list1 = lists.tile([P, SLOTS // 16], U16, name="list1")
@@ -83,19 +85,23 @@ def tile_attend_pairreads_heads_kernel(tc, query, keys_words, keys_scales, lam, 
         make_identity(nc, ident[:])
 
         q_bf = tile("q_bf", [P, Q, PACK], BF16)
-        nc.vector.tensor_copy(
-            q_bf[:].rearrange("p (c i) j -> p c j i", i=4),
-            q_raw[:].rearrange("p j (c i) -> p c j i", i=4),
-        )
+        q_halves = [slice(u * Q // 2, (u + 1) * Q // 2) for u in range(2)]
+        for cols in q_halves:
+            nc.vector.tensor_copy(
+                q_bf[:, cols].rearrange("p (c i) j -> p c j i", i=4),
+                q_raw[:, :, cols].rearrange("p j (c i) -> p c j i", i=4),
+            )
         q_codes = tile("q_codes", [P, Q], U32)
         q_scales = tile("q_scales", [P, Q], U8)
-        nc.vector.quantize_mx(q_codes[:].bitcast(FP8X4), q_scales[:], q_bf[:].rearrange("p q j -> p (q j)"))
+        for cols in q_halves:
+            nc.vector.quantize_mx(q_codes[:, cols].bitcast(FP8X4), q_scales[:, cols], q_bf[:, cols].rearrange("p q j -> p (q j)"))
+
         lam_wide = tile("lam_wide", [P, SLOTS], F32)
         nc.scalar.copy(lam_wide[:], lam_col[:].to_broadcast([P, SLOTS]))
 
         a = tile("a", [P, T], F32)
         for c in range(T // CHUNK):
-            bank = psum.tile([P, CHUNK], F32, name="a_bank%d" % c)
+            bank = psum.tile([P, CHUNK], F32, name="a_bank%d" % c, tag="a_bank%d" % c)
             cols = slice((c % 2) * CHUNK, (c % 2 + 1) * CHUNK)
             nc.tensor.matmul_mx(
                 bank[:],
@@ -117,9 +123,6 @@ def tile_attend_pairreads_heads_kernel(tc, query, keys_words, keys_scales, lam, 
                 v_raw[g, h][:].rearrange("p j (c i) -> p c j i", i=4),
             )
 
-        v_first = tile("v_first", [P, CHUNK, PACK], BF16, "k_words1")
-        interleave_vals(v_first[:], 0, 0)
-
         half = SLOTS // 2
         halves = [(slice(u * half, (u + 1) * half), slice(u * half // 16, (u + 1) * half // 16)) for u in range(2)]
         second = tile("second", [P, SLOTS], F32)
@@ -128,6 +131,8 @@ def tile_attend_pairreads_heads_kernel(tc, query, keys_words, keys_scales, lam, 
             nc.vector.tensor_tensor(second[:, cols], a[:].indirect(list2[:, entries]), lam_wide[:, cols], ALU.mult)
         for cols, entries in halves:
             nc.vector.tensor_tensor(s[:, cols], a[:].indirect(list1[:, entries]), second[:, cols], ALU.add)
+        v_first = tile("v_first", [P, CHUNK, PACK], BF16, "k_words1")
+        interleave_vals(v_first[:], 0, 0)
         neg_max = tile("neg_max", [P, 1], F32)
         nc.vector.tensor_reduce(neg_max[:], s[:], AX.X, ALU.max, negate=True)
         v_codes0 = tile("v_codes0", [P, CHUNK], U32, "second")
@@ -141,7 +146,7 @@ def tile_attend_pairreads_heads_kernel(tc, query, keys_words, keys_scales, lam, 
         nc.scalar.activation(p, s[:], ACT.Exp, bias=neg_max[:], accum_out=total[:])
         v_rest = tile("v_rest", [P, 3 * CHUNK, PACK], BF16, "s")
         interleave_vals(v_rest[:, 0:CHUNK], 0, 1)
-        interleave_vals(v_rest[:, CHUNK : 2 * CHUNK], 1, 0)
+        interleave_vals(v_rest[:, CHUNK : CHUNK + V_CUTS[1][1]], 1, 0)
 
         rinv = tile("rinv", [P, 1], F32)
         nc.vector.tensor_copy(wa[:].indirect(list1[:, 0 : HEAD // 16]), p_head)
@@ -149,6 +154,9 @@ def tile_attend_pairreads_heads_kernel(tc, query, keys_words, keys_scales, lam, 
         nc.vector.reciprocal(rinv[:], total[:])
         nc.vector.tensor_copy(wa[:].indirect(list1[:, HEAD // 16 : SLOTS // 16]), p[:, HEAD:SLOTS])
         nc.vector.tensor_copy(wb[:].indirect(list2[:, HEAD // 16 : SLOTS // 16]), p[:, HEAD:SLOTS])
+        v_codes1 = tile("v_codes1", [P, CHUNK], U32, "total")
+        v_scales1 = tile("v_scales1", [P, CHUNK], U8)
+        nc.vector.quantize_mx(v_codes1[:].bitcast(FP8X4), v_scales1[:], v_rest[:, 0:CHUNK].rearrange("p e j -> p (e j)"))
         rshare = tile("rshare", [P, 1], F32)
         nc.scalar.activation(rshare[:], rinv[:], ACT.Copy, scale=share_col[:])
 
@@ -164,22 +172,32 @@ def tile_attend_pairreads_heads_kernel(tc, query, keys_words, keys_scales, lam, 
             nc.scalar.activation(by_line(wa_dealt[:, g]), by_place(wa, g), ACT.Copy, scale=rinv[:])
             for j in range(PACK):
                 nc.tensor.matmul(wt_banks[g][:, j, :], wa_dealt[:, g, j, :], ident[:], is_transpose=True, start=(j == 0), stop=False)
-        interleave_vals(v_rest[:, 2 * CHUNK : 3 * CHUNK], 1, 1)
+        interleave_vals(v_rest[:, CHUNK + V_CUTS[1][1] : 3 * CHUNK], 1, 1)
 
-        wb_dealt = [tile("wb_dealt0", [P, PACK, P], F32), tile("wb_dealt1", [P, PACK, P], F32, "v_raw11")]
-        nc.vector.tensor_scalar(by_line(wb_dealt[0][:]), by_place(wb, 0), rshare[:], None, ALU.mult)
-        nc.scalar.activation(by_line(wb_dealt[1][:]), by_place(wb, 1), ACT.Copy, scale=rshare[:])
+        wb_dealt = {}
+        for g in range(PASSES):
+            for pair in range(2):
+                dealt = tile("wb_dealt%d%d" % (g, pair), [P, 2, P], F32, "v_raw11" if (g, pair) == (0, 0) else None)
+                source = by_place(wb, g)[:, :, 2 * pair : 2 * pair + 2, :]
+                if (g, pair) != (0, 1):
+                    nc.scalar.activation(by_line(dealt[:]), source, ACT.Copy, scale=rshare[:])
+                else:
+                    nc.vector.tensor_scalar(by_line(dealt[:]), source, rshare[:], None, ALU.mult)
+                wb_dealt[g, pair] = dealt
         for g in range(PASSES):
             for j in range(PACK):
-                nc.tensor.matmul(wt_banks[g][:, j, :], wb_dealt[g][:, j, :], ident[:], is_transpose=True, start=False, stop=(j == PACK - 1))
+                nc.tensor.matmul(wt_banks[g][:, j, :], wb_dealt[g, j // 2][:, j % 2, :], ident[:], is_transpose=True, start=False, stop=(j == PACK - 1))
 
-        v_codes1 = tile("v_codes1", [P, 3 * CHUNK], U32, "v_raw00")
-        v_scales1 = tile("v_scales1", [P, 3 * CHUNK], U8)
-        for lo, hi in ((0, CHUNK), (CHUNK, 3 * CHUNK)):
-            nc.vector.quantize_mx(v_codes1[:, lo:hi].bitcast(FP8X4), v_scales1[:, lo:hi], v_rest[:, lo:hi].rearrange("p e j -> p (e j)"))
-        v_parts = [(v_codes0[:], v_scales0[:])] + [
-            (v_codes1[:, n * CHUNK : (n + 1) * CHUNK], v_scales1[:, n * CHUNK : (n + 1) * CHUNK]) for n in range(3)
-        ]
+        v_codes2 = tile("v_codes2", [P, E], U32, "v_raw00")
+        v_scales2 = tile("v_scales2", [P, E], U8)
+        nc.vector.quantize_mx(v_codes2[:].bitcast(FP8X4), v_scales2[:], v_rest[:, CHUNK : 3 * CHUNK].rearrange("p e j -> p (e j)"))
+
+        def v_part(g, lo, hi):
+            if g == 1:
+                return v_codes2[:, lo:hi], v_scales2[:, lo:hi]
+            if lo < CHUNK:
+                return v_codes0[:, lo:hi], v_scales0[:, lo:hi]
+            return v_codes1[:, lo - CHUNK : hi - CHUNK], v_scales1[:, lo - CHUNK : hi - CHUNK]
 
         wt_bf = [tile("wt_bf%d" % g, [P, Q, PACK], BF16) for g in range(PASSES)]
         for g in range(PASSES):
@@ -191,13 +209,14 @@ def tile_attend_pairreads_heads_kernel(tc, query, keys_words, keys_scales, lam, 
             )
         w_codes = [tile("w_codes%d" % g, [P, Q], U32) for g in range(PASSES)]
         w_scales = [tile("w_scales%d" % g, [P, Q], U8) for g in range(PASSES)]
-        out_banks = [psum.tile([P, CHUNK], F32, name="out_bank%d" % h) for h in range(2)]
+        pieces = [(0, 256), (256, 384), (384, 512)]
+        out_banks = [psum.tile([P, hi - lo], F32, name="out_bank%d" % n, tag="a_bank%d" % n) for n, (lo, hi) in enumerate(pieces)]
         for g in range(PASSES):
             nc.vector.quantize_mx(w_codes[g][:].bitcast(FP8X4), w_scales[g][:], wt_bf[g][:].rearrange("p q j -> p (q j)"))
-            for h in range(2):
-                codes, scales = v_parts[2 * g + h]
+            for bank, (lo, hi) in zip(out_banks, pieces):
+                codes, scales = v_part(g, lo, hi)
                 nc.tensor.matmul_mx(
-                    out_banks[h][:],
+                    bank[:],
                     lhsT=w_codes[g][:].bitcast(FP8X4),
                     lhsT_scale=w_scales[g][:],
                     rhs=codes.bitcast(FP8X4),
@@ -205,9 +224,11 @@ def tile_attend_pairreads_heads_kernel(tc, query, keys_words, keys_scales, lam, 
                     start=(g == 0),
                     stop=(g == PASSES - 1),
                 )
-        res0 = tile("res0", [P, CHUNK], F32)
-        nc.scalar.copy(res0[:], out_banks[0][:])
-        nc.scalar.dma_start(out[:, 0:CHUNK], res0[:])
-        res1 = tile("res1", [P, CHUNK], F32)
-        nc.vector.tensor_copy(res1[:], out_banks[1][:])
-        nc.sync.dma_start(out[:, CHUNK:E], res1[:])
+        for n, (lo, hi) in enumerate(pieces):
+            res = tile("res%d" % n, [P, hi - lo], F32)
+            if n == 0:
+                nc.scalar.copy(res[:], out_banks[n][:])
+                nc.scalar.dma_start(out[:, lo:hi], res[:])
+            else:
+                nc.vector.tensor_copy(res[:], out_banks[n][:])
+                nc.sync.dma_start(out[:, lo:hi], res[:])

@@ -36,7 +36,7 @@ def tile_attend_pairreads_heads_kernel(tc, query, keys_words, keys_scales, lam, 
             return sb.tile(shape, dtype, name=name, tag=tag or name, align_bytes=64)
 
         k_scales = tile("k_scales", [P, CHUNK], U8)
-        nc.vector.memset(k_scales[:].bitcast(I32), 0)
+        nc.gpsimd.memset(k_scales[:].bitcast(I32), 0)
         q_raw = tile("q_raw", [P, PACK, Q], F32)
         nc.sync.dma_start(q_raw[:], query.rearrange("(p j) q -> p j q", j=PACK))
         lam_col = tile("lam_col", [P, 1], F32)
@@ -200,19 +200,23 @@ def tile_attend_pairreads_heads_kernel(tc, query, keys_words, keys_scales, lam, 
             return v_codes1[:, lo - CHUNK : hi - CHUNK], v_scales1[:, lo - CHUNK : hi - CHUNK]
 
         wt_bf = [tile("wt_bf%d" % g, [P, Q, PACK], BF16) for g in range(PASSES)]
-        for g in range(PASSES):
-            nc.vector.tensor_tensor(
-                wt_bf[g][:],
-                wt_banks[g][:].rearrange("p j q -> p q j"),
-                fac_t[:, g, :].unsqueeze(1).to_broadcast([P, Q, PACK]),
-                ALU.mult,
-            )
         w_codes = [tile("w_codes%d" % g, [P, Q], U32) for g in range(PASSES)]
         w_scales = [tile("w_scales%d" % g, [P, Q], U8) for g in range(PASSES)]
         pieces = [(0, 256), (256, 384), (384, 512)]
         out_banks = [psum.tile([P, hi - lo], F32, name="out_bank%d" % n, tag="a_bank%d" % n) for n, (lo, hi) in enumerate(pieces)]
-        for g in range(PASSES):
-            nc.vector.quantize_mx(w_codes[g][:].bitcast(FP8X4), w_scales[g][:], wt_bf[g][:].rearrange("p q j -> p (q j)"))
+
+        def weigh(g, lo, hi):
+            nc.vector.tensor_tensor(
+                wt_bf[g][:, lo:hi],
+                wt_banks[g][:, :, lo:hi].rearrange("p j q -> p q j"),
+                fac_t[:, g, :].unsqueeze(1).to_broadcast([P, hi - lo, PACK]),
+                ALU.mult,
+            )
+
+        def quantise(g, lo, hi):
+            nc.vector.quantize_mx(w_codes[g][:, lo:hi].bitcast(FP8X4), w_scales[g][:, lo:hi], wt_bf[g][:, lo:hi].rearrange("p q j -> p (q j)"))
+
+        def multiply(g):
             for bank, (lo, hi) in zip(out_banks, pieces):
                 codes, scales = v_part(g, lo, hi)
                 nc.tensor.matmul_mx(
@@ -224,6 +228,15 @@ def tile_attend_pairreads_heads_kernel(tc, query, keys_words, keys_scales, lam, 
                     start=(g == 0),
                     stop=(g == PASSES - 1),
                 )
+
+        weigh(0, 0, Q)
+        weigh(1, 0, Q // 2)
+        quantise(0, 0, Q)
+        multiply(0)
+        weigh(1, Q // 2, Q)
+        quantise(1, 0, Q // 2)
+        quantise(1, Q // 2, Q)
+        multiply(1)
         for n, (lo, hi) in enumerate(pieces):
             res = tile("res%d" % n, [P, hi - lo], F32)
             if n == 0:

from contextlib import ExitStack

import concourse.mybir as mybir
from concourse.masks import make_identity

F32 = mybir.dt.float32
BF16 = mybir.dt.bfloat16
I32 = mybir.dt.int32
U32 = mybir.dt.uint32
U16 = mybir.dt.uint16
U8 = mybir.dt.uint8
FP8X4 = mybir.dt.float8_e4m3fn_x4
ALU = mybir.AluOpType
ACT = mybir.ActivationFunctionType
AX = mybir.AxisListType

D, T, Q, SLOTS, E = 512, 1024, 128, 512, 512
P = 128
PACK = 4
K_PASS = P * PACK
PASSES = T // K_PASS
CHUNK = 256
HEAD = 128
V_CUTS = ((0, CHUNK, E), (0, 352, E))
FLOPS = 2 * D * Q * T + 2 * T * Q * E


def tile_attend_pairreads_heads_kernel(tc, query, keys_words, keys_scales, lam, share, fac, vals, offs, offs2, out):
    nc = tc.nc
    with ExitStack() as ctx:
        lists = ctx.enter_context(tc.tile_pool(name="lists", bufs=1))
        sb = ctx.enter_context(tc.tile_pool(name="sb", bufs=1))
        psum = ctx.enter_context(tc.psum_pool(name="psum", bufs=1))

        def tile(name, shape, dtype, tag=None):
            return sb.tile(shape, dtype, name=name, tag=tag or name, align_bytes=64)

        k_scales = tile("k_scales", [P, CHUNK], U8)
        nc.gpsimd.memset(k_scales[:].bitcast(I32), 0)
        q_raw = tile("q_raw", [P, PACK, Q], F32)
        nc.sync.dma_start(q_raw[:], query.rearrange("(p j) q -> p j q", j=PACK))
        lam_col = tile("lam_col", [P, 1], F32)
        nc.sync.dma_start(lam_col[:], lam)
        for quad in range(4):
            rows = keys_scales[0, 4 * quad : 4 * quad + 4, :].bitcast(I32)
            nc.scalar.dma_start(
                k_scales[32 * quad : 32 * quad + 16, :].bitcast(I32),
                rows.rearrange("r (c n) -> c r n", c=T // CHUNK),
            )
        words = keys_words[0].rearrange("p n t -> p (n t)").bitcast(I32)
        k_words = []
        for h in range(2):
            kw = tile("k_words%d" % h, [P, T // 2], U32)
            nc.sync.dma_start(kw[:].bitcast(I32), words[:, h * (T // 2) : (h + 1) * (T // 2)])
            k_words.append(kw)
        list2 = lists.tile([P, SLOTS // 16], U16, name="list2")
        nc.sync.dma_start(list2[:], offs2)
        v_raw = {}

        def load_vals(g, h):
            lo, hi = V_CUTS[g][h], V_CUTS[g][h + 1]
            v_raw[g, h] = tile("v_raw%d%d" % (g, h), [P, PACK, hi - lo], F32)
            part = vals[g * K_PASS : (g + 1) * K_PASS, lo:hi]
            nc.sync.dma_start(v_raw[g, h][:], part.rearrange("(p j) e -> p j e", j=PACK))

        list1 = lists.tile([P, SLOTS // 16], U16, name="list1")
        nc.sync.dma_start(list1[:], offs)
        load_vals(0, 0)
        load_vals(0, 1)
        load_vals(1, 0)
        load_vals(1, 1)
        share_col = tile("share_col", [P, 1], F32)
        nc.sync.dma_start(share_col[:], share)
        fac_t = tile("fac_t", [P, PASSES, PACK], F32)
        nc.sync.dma_start(fac_t[:], fac[0].rearrange("(g p j) -> p g j", g=PASSES, j=PACK))

        warm = tile("warm", [P, 2], F32)
        nc.vector.memset(warm[:, 0:1], 0.0)
        nc.scalar.activation(warm[:, 1:2], warm[:, 0:1], ACT.Exp)
        wa = tile("wa", [P, T], F32)
        wb = tile("wb", [P, T], F32)
        nc.vector.memset(wa[:], 0.0)
        nc.vector.memset(wb[:], 0.0)
        ident = tile("ident", [P, P], F32)
        make_identity(nc, ident[:])

        q_bf = tile("q_bf", [P, Q, PACK], BF16)
        q_halves = [slice(u * Q // 2, (u + 1) * Q // 2) for u in range(2)]
        for cols in q_halves:
            nc.vector.tensor_copy(
                q_bf[:, cols].rearrange("p (c i) j -> p c j i", i=4),
                q_raw[:, :, cols].rearrange("p j (c i) -> p c j i", i=4),
            )
        q_codes = tile("q_codes", [P, Q], U32)
        q_scales = tile("q_scales", [P, Q], U8)
        for cols in q_halves:
            nc.vector.quantize_mx(q_codes[:, cols].bitcast(FP8X4), q_scales[:, cols], q_bf[:, cols].rearrange("p q j -> p (q j)"))

        lam_wide = tile("lam_wide", [P, SLOTS], F32)
        nc.scalar.copy(lam_wide[:], lam_col[:].to_broadcast([P, SLOTS]))

        a = tile("a", [P, T], F32)
        for c in range(T // CHUNK):
            bank = psum.tile([P, CHUNK], F32, name="a_bank%d" % c, tag="a_bank%d" % c)
            cols = slice((c % 2) * CHUNK, (c % 2 + 1) * CHUNK)
            nc.tensor.matmul_mx(
                bank[:],
                lhsT=q_codes[:].bitcast(FP8X4),
                lhsT_scale=q_scales[:],
                rhs=k_words[c // 2][:, cols].bitcast(FP8X4),
                rhs_scale=k_scales[4 * c : P, :],
                start=True,
                stop=True,
            )
            if c % 2 == 0:
                nc.vector.tensor_copy(a[:, c * CHUNK : (c + 1) * CHUNK], bank[:])
            else:
                nc.scalar.copy(a[:, c * CHUNK : (c + 1) * CHUNK], bank[:])

        def interleave_vals(dst, g, h):
            nc.scalar.copy(
                dst.rearrange("p (c i) j -> p c j i", i=4),
                v_raw[g, h][:].rearrange("p j (c i) -> p c j i", i=4),
            )

        half = SLOTS // 2
        halves = [(slice(u * half, (u + 1) * half), slice(u * half // 16, (u + 1) * half // 16)) for u in range(2)]
        second = tile("second", [P, SLOTS], F32)
        s = tile("s", [P, SLOTS], F32)
        for cols, entries in halves:
            nc.vector.tensor_tensor(second[:, cols], a[:].indirect(list2[:, entries]), lam_wide[:, cols], ALU.mult)
        for cols, entries in halves:
            nc.vector.tensor_tensor(s[:, cols], a[:].indirect(list1[:, entries]), second[:, cols], ALU.add)
        v_first = tile("v_first", [P, CHUNK, PACK], BF16, "k_words1")
        interleave_vals(v_first[:], 0, 0)
        neg_max = tile("neg_max", [P, 1], F32)
        nc.vector.tensor_reduce(neg_max[:], s[:], AX.X, ALU.max, negate=True)
        v_codes0 = tile("v_codes0", [P, CHUNK], U32, "second")
        v_scales0 = tile("v_scales0", [P, CHUNK], U8)
        nc.vector.quantize_mx(v_codes0[:].bitcast(FP8X4), v_scales0[:], v_first[:].rearrange("p e j -> p (e j)"))

        p_both = tile("p_both", [P, HEAD + SLOTS], F32, "v_raw00")
        p_head, p = p_both[:, 0:HEAD], p_both[:, HEAD : HEAD + SLOTS]
        nc.scalar.activation(p_head, s[:, 0:HEAD], ACT.Exp, bias=neg_max[:])
        total = tile("total", [P, 1], F32)
        nc.scalar.activation(p, s[:], ACT.Exp, bias=neg_max[:], accum_out=total[:])
        v_rest = tile("v_rest", [P, 3 * CHUNK, PACK], BF16, "s")
        interleave_vals(v_rest[:, 0:CHUNK], 0, 1)
        interleave_vals(v_rest[:, CHUNK : CHUNK + V_CUTS[1][1]], 1, 0)

        rinv = tile("rinv", [P, 1], F32)
        nc.vector.tensor_copy(wa[:].indirect(list1[:, 0 : HEAD // 16]), p_head)
        nc.vector.tensor_copy(wb[:].indirect(list2[:, 0 : HEAD // 16]), p_head)
        nc.vector.reciprocal(rinv[:], total[:])
        nc.vector.tensor_copy(wa[:].indirect(list1[:, HEAD // 16 : SLOTS // 16]), p[:, HEAD:SLOTS])
        nc.vector.tensor_copy(wb[:].indirect(list2[:, HEAD // 16 : SLOTS // 16]), p[:, HEAD:SLOTS])
        v_codes1 = tile("v_codes1", [P, CHUNK], U32, "total")
        v_scales1 = tile("v_scales1", [P, CHUNK], U8)
        nc.vector.quantize_mx(v_codes1[:].bitcast(FP8X4), v_scales1[:], v_rest[:, 0:CHUNK].rearrange("p e j -> p (e j)"))
        rshare = tile("rshare", [P, 1], F32)
        nc.scalar.activation(rshare[:], rinv[:], ACT.Copy, scale=share_col[:])

        def by_place(window, g):
            return window[:, g * K_PASS : (g + 1) * K_PASS].rearrange("q (c i j) -> q c j i", i=4, j=PACK)

        def by_line(dealt):
            return dealt.rearrange("q j (c i) -> q c j i", i=4)

        wa_dealt = tile("wa_dealt", [P, PASSES, PACK, P], F32, "v_raw10")
        wt_banks = [psum.tile([P, PACK, Q], F32, name="wt_bank%d" % g) for g in range(PASSES)]
        for g in range(PASSES):
            nc.scalar.activation(by_line(wa_dealt[:, g]), by_place(wa, g), ACT.Copy, scale=rinv[:])
            for j in range(PACK):
                nc.tensor.matmul(wt_banks[g][:, j, :], wa_dealt[:, g, j, :], ident[:], is_transpose=True, start=(j == 0), stop=False)
        interleave_vals(v_rest[:, CHUNK + V_CUTS[1][1] : 3 * CHUNK], 1, 1)

        wb_dealt = {}
        for g in range(PASSES):
            for pair in range(2):
                dealt = tile("wb_dealt%d%d" % (g, pair), [P, 2, P], F32, "v_raw11" if (g, pair) == (0, 0) else None)
                source = by_place(wb, g)[:, :, 2 * pair : 2 * pair + 2, :]
                if (g, pair) != (0, 1):
                    nc.scalar.activation(by_line(dealt[:]), source, ACT.Copy, scale=rshare[:])
                else:
                    nc.vector.tensor_scalar(by_line(dealt[:]), source, rshare[:], None, ALU.mult)
                wb_dealt[g, pair] = dealt
        for g in range(PASSES):
            for j in range(PACK):
                nc.tensor.matmul(wt_banks[g][:, j, :], wb_dealt[g, j // 2][:, j % 2, :], ident[:], is_transpose=True, start=False, stop=(j == PACK - 1))

        v_codes2 = tile("v_codes2", [P, E], U32, "v_raw00")
        v_scales2 = tile("v_scales2", [P, E], U8)
        nc.vector.quantize_mx(v_codes2[:].bitcast(FP8X4), v_scales2[:], v_rest[:, CHUNK : 3 * CHUNK].rearrange("p e j -> p (e j)"))

        def v_part(g, lo, hi):
            if g == 1:
                return v_codes2[:, lo:hi], v_scales2[:, lo:hi]
            if lo < CHUNK:
                return v_codes0[:, lo:hi], v_scales0[:, lo:hi]
            return v_codes1[:, lo - CHUNK : hi - CHUNK], v_scales1[:, lo - CHUNK : hi - CHUNK]

        wt_bf = [tile("wt_bf%d" % g, [P, Q, PACK], BF16) for g in range(PASSES)]
        w_codes = [tile("w_codes%d" % g, [P, Q], U32) for g in range(PASSES)]
        w_scales = [tile("w_scales%d" % g, [P, Q], U8) for g in range(PASSES)]
        pieces = [(0, 256), (256, 384), (384, 512)]
        out_banks = [psum.tile([P, hi - lo], F32, name="out_bank%d" % n, tag="a_bank%d" % n) for n, (lo, hi) in enumerate(pieces)]

        def weigh(g, lo, hi):
            nc.vector.tensor_tensor(
                wt_bf[g][:, lo:hi],
                wt_banks[g][:, :, lo:hi].rearrange("p j q -> p q j"),
                fac_t[:, g, :].unsqueeze(1).to_broadcast([P, hi - lo, PACK]),
                ALU.mult,
            )

        def quantise(g, lo, hi):
            nc.vector.quantize_mx(w_codes[g][:, lo:hi].bitcast(FP8X4), w_scales[g][:, lo:hi], wt_bf[g][:, lo:hi].rearrange("p q j -> p (q j)"))

        def multiply(g):
            for bank, (lo, hi) in zip(out_banks, pieces):
                codes, scales = v_part(g, lo, hi)
                nc.tensor.matmul_mx(
                    bank[:],
                    lhsT=w_codes[g][:].bitcast(FP8X4),
                    lhsT_scale=w_scales[g][:],
                    rhs=codes.bitcast(FP8X4),
                    rhs_scale=scales,
                    start=(g == 0),
                    stop=(g == PASSES - 1),
                )

        weigh(0, 0, Q)
        weigh(1, 0, Q // 2)
        quantise(0, 0, Q)
        multiply(0)
        weigh(1, Q // 2, Q)
        quantise(1, 0, Q // 2)
        quantise(1, Q // 2, Q)
        multiply(1)
        for n, (lo, hi) in enumerate(pieces):
            res = tile("res%d" % n, [P, hi - lo], F32)
            if n == 0:
                nc.scalar.copy(res[:], out_banks[n][:])
                nc.scalar.dma_start(out[:, lo:hi], res[:])
            else:
                nc.vector.tensor_copy(res[:], out_banks[n][:])
                nc.sync.dma_start(out[:, lo:hi], res[:])
